import numpy as np, ml_dtypes
CORES = [242,247,114,119]
N = 4
BF = ml_dtypes.bfloat16
W, H, Q, L, V, TH, TH2 = 4096, 256, 16, 2, 4, 1082, 820
J = Q - L + 1
HALF = (J - 1) // 2
B = HALF + L - 1
def which(s, z):
    return np.maximum(1, np.add.reduce((s <= z[:, None, :]).astype(np.int64), axis=1)) - 1
def place(s, c, k, p):
    sk = np.take_along_axis(s, k[:, None, :], 1); ck = np.take_along_axis(c, k[:, None, :], 1)
    return ((p - sk) * (2 * ck + 1) + 37 * ck) & (W - 1)
def pick(x, f):
    return np.take_along_axis(x, f.reshape(8, 1, -1), 2).reshape(8, 16, -1, H)
def seen(x, s, c, z):
    o = (5 * np.arange(H)) & (H - 1); got = []
    for q in range(N):
        so = s[q][..., o]; co = c[q][..., o]
        got.append(pick(x[q], place(so, co, which(so, z[q]), z[q][:, None, :] + np.arange(Q)[None, :, None] - B)))
    return np.stack(got)
def parts(rng):
    span = rng.integers(116, 141, (N, 8, 1, 1))
    x = 128 + np.floor((rng.random((N, 8, 16, W), dtype=np.float32) - 0.5) * span).astype(np.int64)
    tm = 128 + np.floor((rng.random((N, 8, 16, L, H)) - 0.5) * span[..., None]).astype(np.int64)
    s = np.sort(rng.integers(0, W, (N, 8, 16, H)), axis=2); c = rng.integers(0, 1024, (N, 8, 16, H)); z = rng.integers(16, 3001, (N, 8, H))
    return x, s, c, z, tm
def pack(x, s, c, z, tm):
    return {"xl": np.ascontiguousarray(x).reshape(N, 128, W).astype(np.float32).astype(BF), "s0": np.ascontiguousarray(s).reshape(N, 128, H).astype(np.int32),
            "cf": np.ascontiguousarray(c).reshape(N, 128, H).astype(np.int32), "z0": np.ascontiguousarray(z).astype(np.int32),
            "t0": np.ascontiguousarray(tm).reshape(N, 128, L * H).astype(np.float32).astype(BF)}
def setup_inputs(rng):
    return pack(*parts(rng))
def setup_inputs_spread(rng):
    amps = np.array([4, 16, 32, 64, 96, 128])
    x = np.clip(128 + np.floor((2 * rng.random((N, 8, 16, W), dtype=np.float32) - 1) * rng.choice(amps, (N, 8, 1, W))), 0, 255).astype(np.int64)
    tm = np.clip(128 + np.floor((2 * rng.random((N, 8, 16, L, H)) - 1) * rng.choice(amps, (N, 8, 1, L, H))), 0, 255).astype(np.int64)
    s = np.where(rng.random((N, 8, 1, H)) < 0.5, rng.integers(0, W, (N, 8, 16, H)), np.clip(np.floor(np.exp2(12 * rng.random((N, 8, 16, H)))).astype(np.int64) - 1, 0, W - 1))
    c = np.clip(np.floor(np.exp2(10 * rng.random((N, 8, 16, H)))).astype(np.int64) - 1, 0, 1023)
    z = np.where(rng.random((N, 8, H)) < 0.5, rng.integers(16, 3001, (N, 8, H)), np.clip(np.floor(np.exp2(11.6 * rng.random((N, 8, H)))).astype(np.int64), 16, 3000))
    return pack(x, np.sort(s, axis=2), c, z, tm)
def turns(w, u):
    return np.where((u & 1) == 1, 255 - w, w)
def setup_inputs_ends(rng):
    x = 255 * (rng.random((N, 8, 16, W), dtype=np.float32) < 0.125).astype(np.int64); tm = 255 * (rng.random((N, 8, 16, L, H)) < 0.125).astype(np.int64)
    flip = rng.permutation(np.array([0, 0, 1, 1]))
    for g in range(2, 6):
        if flip[g - 2] == 1: x[:, g] = 255 - x[:, g]; tm[:, g] = 255 - tm[:, g]
    nz = rng.integers(0, 17, (N, 8, 1, H)); low = np.where(np.arange(16).reshape(1, 1, 16, 1) < nz, 0, W - 1)
    s = np.where(rng.random((N, 8, 1, H)) < 0.5, low, (W - 1) * rng.integers(0, 2, (N, 8, 16, H))); s[..., 0] = 0; s[..., H - 1] = W - 1
    c = 1023 * rng.integers(0, 2, (N, 8, 16, H)); z = 16 + 2984 * rng.integers(0, 2, (N, 8, H)); z[..., 0] = 16; z[..., H - 1] = 3000
    level = 255 * int(rng.integers(0, 2)); turn = int(rng.integers(0, 2))
    x[:, 7] = level; rec = 255 * rng.integers(0, 2, (N, 1, 1, H)); rec[..., 0] = 255 - level; rec[..., H - 1] = 255 - level; rec[..., 1] = level; rec[..., H - 2] = level; tm[:, 7] = rec
    for q in range(N): x[q, 0] = 255 * ((q + turn) % 2)
    tm[:, 0] = 255 * rng.integers(0, 2, (N, 1, 1, H))
    x[:, 1, :, 0::2] = 0; x[:, 1, :, 1::2] = 255; tm[:, 1] = 255 * rng.integers(0, 2, (N, 1, L, H))
    code = 255 * rng.integers(0, 2, (16, HALF * N))
    for q in range(N): x[q, 6] = code[:, (np.arange(W) - HALF * q) % (HALF * N)]
    s[:, 6] = 0; c[:, 6] = 0
    b = int(rng.integers(0, N)); s[:, 5] = W - 1; c[:, 5] = 1023; z[:, 5] = 3000; z[b, 5] = 16
    u = np.arange(W) - 4300; col = (u * 2047 + 37 * 1023) & (W - 1)
    far = W - 1 + HALF * (V - 1 - (V - 1) // N)
    p = 255 * rng.integers(0, 2, (16, 1)); other = np.where(rng.permutation(16).reshape(16, 1) < 8, 255 - p, p)
    period = HALF * (N - 1); ring = 255 * rng.integers(0, 2, (16, period)); ring[:, int(u[np.argmin(col)]) % period] = (255 - turns(p, far - HALF))[:, 0]
    for d in range(N):
        near = turns(p if d % 2 == 0 else other, u)
        if d == N - 1: near = np.where((u >= -far - HALF) & (u < -far - HALF + L), turns(p, u), near)
        x[(b + d) % N, 5][:, col] = np.where(u < -2600, near, ring[:, (u + HALF * d) % period])
    y = seen(x, s, c, z)
    tm[:, 6] = y[:, 6, :, J - 1:J - 1 + L]; tm[:, 5] = y[:, 5, :, :L]; tm[b, 5] = turns(other, np.arange(L))[:, :, None]
    return pack(x, s, c, z, tm)
def setup_inputs_corners(rng):
    x, s1, c, z, tm = parts(rng); gs = rng.permutation(8)
    x[:, gs[0]] = 120 + (x[:, gs[0]] & 15); x[:, gs[1]] = rng.integers(0, 256, (N, 16, W))
    kind = rng.integers(0, 8, (N, 8, 1, H)); s = np.where(kind == 1, s1[:, :, 5:6], s1); s = np.where(kind == 2, s1[:, :, ::-1], s); s = np.where(kind == 3, W - 1, s)
    s = np.where(kind == 4, np.arange(16).reshape(1, 1, 16, 1), s); s = np.where(kind == 5, rng.permuted(s1, axis=2), s)
    c = np.where(rng.random((N, 8, 16, H)) < 0.3, rng.choice(np.array([0, 1, 511, 512, 1023]), (N, 8, 16, H)), c)
    so = s[..., (5 * np.arange(H)) & (H - 1)]; near = np.take_along_axis(so, rng.integers(0, 16, (N, 8, 1, H)), 2)[:, :, 0]
    z = np.clip(near + rng.choice(np.array([-6, -1, 0, 1, 5, Q - 1, Q, Q + 1]), (N, 8, H)), 16, 3000)
    y = seen(x, s, c, z); j0 = rng.choice(np.array([0, 1, HALF, J - 1]), (N, 8, 1, 1, H)); m = np.take_along_axis(y, j0 + np.arange(L).reshape(1, 1, 1, L, 1), 3)
    tm = np.where(rng.random((N, 8, 1, 1, H)) < 0.6, m, tm)
    tm[:, gs[2]] = 255 * rng.integers(0, 2, (N, 1, L, H)); tm[:, gs[3]] = m[:, gs[3]]
    tm[:, gs[4]] = 255 * rng.integers(0, 2, (N, 1, L, H)); tm[:, gs[4], :, :, H - 1] = m[:, gs[4], :, :, H - 1]
    return pack(x, s, c, z, tm)
def steps(rng):
    b = TH2 // 16; e = rng.integers(-8, 9, 8)
    return b + np.concatenate([e, -e]) + (np.arange(16) < TH2 - 16 * b).astype(np.int64)
def pairs(rng, total, w):
    a = np.zeros(16, np.int64); a[[0, 9]] = (w + 1) // 2; a[[1, 8]] = w // 2
    rest = total - 2 * w; b = rest // 12; e = rng.integers(-8, 9, 6)
    a[[2, 3, 4, 5, 6, 7, 10, 11, 12, 13, 14, 15]] = b + np.concatenate([e, -e]) + (np.arange(12) < rest - 12 * b).astype(np.int64)
    return a
def setup_inputs_edges(rng):
    x, s, c, z, tm = parts(rng)
    for g in range(8):
        if g % 4 == 1: continue
        p0 = rng.integers(50, 71, 16); p1 = p0 + steps(rng); p2 = p1 + steps(rng); p3 = p2 - steps(rng); p3[int(rng.integers(0, 16))] -= 1
        p = np.stack([p0, p1, p2, p3], axis=1)
        for q in range(N): x[q, g] = p[:, (np.arange(W) + int(rng.integers(0, 4))) & 3]
    w = 257 + 4 * int(rng.integers(0, 6)); p0 = rng.integers(20, 61, 16); p1 = p0 + pairs(rng, TH2 + 1, w); p2 = p1 + rng.integers(1, 4, 16); p3 = p2 - pairs(rng, TH2, w + 2)
    p = np.stack([p0, p1, p2, p3], axis=1)
    for q in range(N): x[q, 5] = p[:, (np.arange(W) + int(rng.integers(0, 4))) & 3]
    y = seen(x, s, c, z); dist = rng.choice(np.array([0, TH - 1, TH, TH + 1]), (N, 8, 1, 1, H)); j0 = rng.integers(0, 4, (N, 8, 1, 1, H))
    m = np.take_along_axis(y, j0 + np.arange(L).reshape(1, 1, 1, L, 1), 3); each = dist // (16 * L)
    d = each + (np.arange(16 * L).reshape(1, 1, 16, L, 1) < dist - 16 * L * each)
    sign = np.where(m < 80, -1, np.where(m > 135, 1, 1 - 2 * (np.arange(16).reshape(1, 1, 16, 1, 1) & 1)))
    planted = (np.arange(8) % 4 != 1).reshape(1, 8, 1, 1, 1)
    return pack(x, s, c, z, np.where(planted, m + sign * d, tm))
def check_inputs(d):
    bad = []
    for k, lo, hi in (("xl", 0, 255), ("s0", 0, W - 1), ("cf", 0, 1023), ("z0", 16, 3000), ("t0", 0, 255)):
        a = np.asarray(d[k]).astype(np.float64)
        if not (np.min(a) >= lo and np.max(a) <= hi): bad.append("range of " + k)
        elif np.any(a != np.floor(a)): bad.append("whole numbers in " + k)
    return bad
def reference(xl, s0, cf, z0, t0):
    x = xl.astype(np.int32).reshape(N, 8, 16, W); s = s0.astype(np.int64).reshape(N, 8, 16, H); c = cf.astype(np.int64).reshape(N, 8, 16, H)
    z = z0.astype(np.int64); tm = t0.astype(np.int32).reshape(N, 8, 16, L, H); ties = np.zeros((N, 8), np.int64)
    row = np.arange(16)[None, :, None]; m = np.arange(Q)[None, :, None]
    for t in range(V):
        for r in range(N):
            q = (r + t) % N
            o = ((5 * np.arange(H)[None, :] + ties[r][:, None]) & (H - 1))[:, None, :]
            so = np.take_along_axis(s[q], o, 2); co = np.take_along_axis(c[q], o, 2)
            k = which(so, z[r])
            y = pick(x[q], place(so, co, k, z[r][:, None, :] + m - B))
            e = np.stack([np.add.reduce(np.abs(y[:, :, j:j + L] - tm[r]), axis=(1, 2)) for j in range(J)])
            best = np.argmin(e, axis=0); tie = np.min(e, axis=0) < TH
            so = so + np.where(tie[:, None, :] & (row >= k[:, None, :]), HALF - best[:, None, :], 0)
            np.put_along_axis(s[q], o, so, 2)
            zz = np.where(tie, z[r], np.maximum(z[r] - Q, 0)); k = np.where(tie, k, which(so, zz))
            v = pick(x[q], place(so, co, k, zz[:, None, :] + m))
            over = (np.add.reduce(np.abs(v[:, :, 1:] - v[:, :, :-1]), axis=1) > TH2)[:, L - 1:]
            n = np.where(np.any(over, axis=1), L + np.argmax(over, axis=1), Q)
            tm[r] = np.take_along_axis(v, n[:, None, None, :] - L + np.arange(L)[None, None, :, None], 2)
            z[r] = zz + n - 1
            ties[r] = np.add.reduce(tie.astype(np.int64), axis=1)
    return {"ys": s.reshape(N, 128, H).astype(np.float32), "yz": z.astype(np.float32), "yt": tm.reshape(N, 128, L * H).astype(np.float32).astype(BF)}

@@ -1,0 +1,584 @@
+import numpy as np
+import comms_topo
+from concourse.bass import DstId, RemoteDMATransfer
+from concourse.mybir import dt, AluOpType, AxisListType, ActivationFunctionType
+
+OP = AluOpType
+AF = ActivationFunctionType
+NV, W, ZC, TH, TH2 = 4, 4096, 1536, 1082, 820
+NC = 128
+SYNCNS = 70
+PE_NS = 0.5
+JA = (4, 4)
+YSPLIT = [[("V", 32), ("A", 96)], [("A", 128)]]
+VSPLIT = [[("A", 128)], [("V", 48), ("A", 80)]]
+TQ = ("V", "A")
+DQ = "A"
+BI = {'M1': -7800, 'S0': -3315, 'L1': -6658, 'M0': -4480, 'N1': -6905, 'D1': -5589, 'Q0': -3380, 'A1': -8198, 'Q1': -4886, 'N0': 12695, 'C1': 992, 'S1': -2446, 'R0': -1246, 'A0': -1072, 'V0': -6089, 'Y1': 4200, 'L0': 6209, 'Y0': -679, 'P': -1558, 'D0': 281, 'V1': -1114, 'C0': -2842}
+CORD = (1, 0)
+RECV = 2500
+GN = 1.56
+
+SCRATCH = {}
+
+
+def _b(name, cols, dtype, where="sbuf", rows=128):
+    SCRATCH[name] = (where, [rows, cols], dtype)
+
+
+for _v in range(4):
+    _b("XL%d" % _v, W, "bfloat16")
+    _b("CF%d" % _v, 256, "float32")
+    _b("SX%d" % _v, 257, "float32")
+    _b("SR%d" % (_v + 1), 257, "float32")
+for _n, _c, _d in (("CFI", 256, "int32"), ("S0I", 256, "int32"), ("TT", 512, "bfloat16"), ("YSO", 256, "float32"),
+                   ("SROT0", 256, "float32"), ("SROT1", 256, "float32"), ("D0", 256, "float32"), ("D1", 256, "float32"),
+                   ("CH0", 256, "float16"), ("CH1", 256, "float16"),
+                   ("colI", 128, "int32"), ("cgI", 128, "int32"), ("crI", 128, "int32"),
+                   ("c8", 8, "float32"), ("BLKf", 128, "float32"), ("SEL", 2048, "bfloat16"), ("IDh", 128, "float16"),
+                   ("MMC1", 128, "float16"), ("MMC2", 128, "float16"),
+                   ("G32", 8, "bfloat16"), ("GM16", 8, "bfloat16"), ("G16", 8, "bfloat16"), ("Gn", 8, "bfloat16"), ("G205", 8, "float32"),
+                   ("RST", 128, "float32"), ("ONE", 128, "bfloat16"), ("ONEh", 128, "float16"), ("CROW", 128, "bfloat16"),
+                   ("KT", 8, "bfloat16"),
+                   ("EXz", 128, "float16"), ("EXn", 128, "float16"), ("EXzn", 128, "float16"), ("EXs", 8, "float16"),
+                   ("AP8", 8, "float32"), ("LO", 16, "uint16"), ("LS", 16, "uint16")):
+    _b(_n, _c, _d)
+VIRT = {}
+for _p, _c, _d, _l in (("PF", 1, "float32", "rg rr r7 q3 rp1 rm8 rpos wz wn wm wzn r16 dA"), ("PI", 1, "int32", "rowI rgI rrI r7I q3I"),
+                       ("PJ", 16, "int32", "c16 i16 n205 o5a o5b LA LB LC LD"), ("PG", 128, "float32", "cg cr TRf MA CRW2"),
+                       ("PB", 128, "bfloat16", "BLKb BLKn BM0 BM1 TRI IDb IDn")):
+    for _k, _n in enumerate(_l.split()):
+        VIRT[_n] = (_p, _k * _c, _c)
+    _b(_p, _c * len(_l.split()), _d)
+_b("Z8I", 256, "int32", rows=8)
+_b("Z8", 256, "float16", rows=8)
+_b("YZ", 256, "float32", rows=8)
+for _k in range(2):
+    for _n, _c, _d in (("MASK", NC, "bfloat16"), ("X", NC, "float32"), ("XS", NC, "float32"), ("CS", NC, "float16"),
+                       ("LI", NC, "int32"), ("LJ", NC, "int32"), ("OFF", NC, "uint16"), ("Y", 16 * NC, "bfloat16"),
+                       ("V", 16 * NC, "bfloat16"), ("MX", 30 * NC, "bfloat16"), ("AX", max(1, 2 * max(JA)) * NC, "bfloat16"), ("SC", 128, "float32"), ("KI", 8, "int32"),
+                       ("JJ", 8, "int32"), ("DZ", 8, "float32"), ("ZL", 8, "float32"), ("TD", 8, "float32"),
+                       ("SM", 24, "float16"), ("GE", NC, "float32"), ("AB", 16 * NC, "bfloat16"),
+                       ("OV", NC, "bfloat16"), ("IZ", NC, "bfloat16"), ("TO", 16, "uint16")):
+        _b("%s_%d" % (_n, _k), _c, _d)
+    _b("ST_%d" % _k, NC, "float16", rows=24)
+    for _n in ("K", "T", "E", "V"):
+        _b("p%s%d" % (_n, _k), 512, "float32", where="psum")
+
+SEMAPHORES = ["sV", "sA", "sP", "sG"]
+SEMAPHORES += ["d_" + n for n in ("s0", "cf", "z0", "t00", "t01", "t10", "t11", "xa", "xb", "ys", "yz", "ya0", "ya1", "yb0", "yb1")]
+for _v in range(1, 4):
+    SEMAPHORES += ["%s%d" % (n, _v) for n in ("rca", "rla", "rlb", "lca", "lla", "llb")]
+for _v in range(1, 5):
+    SEMAPHORES += ["%s%d%d" % (n, _v, c) for n in ("rs", "ls") for c in range(2)]
+
+
+class _Plan(dict):
+    pass
+
+
+def plan(g, core, T, topo):
+    rank = T.rank_of(core)
+    n = len(T.cores)
+    ops = []
+    tag = ["c"]
+
+    def B(name):
+        if name in VIRT:
+            p, lo, c = VIRT[name]
+            return (p, lo, lo + c)
+        return (name, 0, SCRATCH[name][1][1])
+
+    def op(q, fns, reads, writes, cost, kind="c", sem=None, cnt=0):
+        ops.append(dict(tag=tag[0], q=q, fns=fns, r=reads, w=writes, cost=cost, kind=kind, sem=sem, cnt=cnt))
+        return len(ops) - 1
+
+    def ap(x):
+        if len(x) == 3:
+            return T[x[0]][:, x[1]:x[2]]
+        if x[3] == "p":
+            return T[x[0]][0:x[4], x[1]:x[2]]
+        return T[x[0]][:, x[1]:x[2]:x[3]]
+
+    def width(x):
+        if len(x) > 3 and x[3] != "p":
+            return -(-(x[2] - x[1]) // x[3])
+        return x[2] - x[1]
+
+    def psum(x):
+        return SCRATCH[x[0]][0] == "psum"
+
+    def reg(x):
+        return (x[0], x[1], x[2])
+
+    def tt(o, a, b, alu):
+        c = width(o) * (1 if psum(a) or psum(b) else 2)
+        op("V", [lambda: g.vector.tensor_tensor(ap(o), ap(a), ap(b), alu)], [reg(a), reg(b)], [reg(o)], max(64, c))
+
+    def sc(x):
+        return ap(x) if isinstance(x, tuple) else x
+
+    def ts(o, a, s1, op0, s2=None, op1=None):
+        rd = [reg(a)] + [reg(s) for s in (s1, s2) if isinstance(s, tuple)]
+        if op1 is None:
+            f = [lambda: g.vector.tensor_scalar(ap(o), ap(a), sc(s1), None, op0)]
+        else:
+            f = [lambda: g.vector.tensor_scalar(ap(o), ap(a), sc(s1), sc(s2), op0, op1)]
+        op("V", f, rd, [reg(o)], max(64, width(o)))
+
+    def cp(o, a):
+        op("V", [lambda: g.vector.tensor_copy(ap(o), ap(a))], [reg(a)], [reg(o)], max(64, width(o)))
+
+    def ms(o, val):
+        op("V", [lambda: g.vector.memset(ap(o), val)], [], [reg(o)], max(64, width(o)))
+
+    def gather(q, o, win, off, scale=1.0, bias=0.0):
+        cost = 60 + GN * width(o)
+        if q == "V":
+            f = lambda: g.vector.tensor_copy(ap(o), ap(win).indirect(ap(off)))
+            if scale != 1.0 or bias != 0.0:
+                f = lambda: g.vector.tensor_scalar(ap(o), ap(win).indirect(ap(off)), scale, bias, OP.mult, OP.add)
+        else:
+            f = lambda: g.scalar.activation(ap(o), ap(win).indirect(ap(off)), AF.Copy)
+            if scale != 1.0 or bias != 0.0:
+                f = lambda: g.scalar.activation(ap(o), ap(win).indirect(ap(off)), AF.Identity, bias=bias, scale=scale)
+        op(q, [f], [reg(win), reg(off)], [reg(o)], cost)
+
+    def mm(o, pairs, start=True, stop=True, wreg=None):
+        fns, rd, cost = [], [], 0
+        for k, (l, r) in enumerate(pairs):
+            fns.append(lambda l=l, r=r, k=k: g.tensor.matmul(ap(o), ap(l), ap(r), start and k == 0, stop and k == len(pairs) - 1))
+            rd += [reg(l), reg(r)]
+            cost += max(min(64, width(l)), width(r)) * (4 if SCRATCH[l[0]][2] == "float32" else 1) * PE_NS
+        op("P", fns, rd, [wreg or reg(o)], cost)
+
+    def dma(q, o, a, rd, wr, sem, cost):
+        eng = g.sync if q == "S" else g.scalar
+        op(q, [lambda: eng.dma_start(o, a)], rd, wr, cost, kind="dma", sem=sem)
+
+    def send(dst, out, src, rs, ls):
+        rid, pid = topo.addr(dst, core)
+        m = topo.mask(core, dst)
+        op("G", [lambda: g.remote_dma(ap(out), ap(src), T.sem[rs], T.sem[ls], pid, rid, m)], [reg(src)], [], 1000,
+           kind="send", sem=ls, cnt=len(topo.engines(core, dst)))
+        return len(ops) - 1
+
+    def recv(o, src, rs, cost, after):
+        op("R", [], [], [reg(o)], cost, kind="recv", sem=rs, cnt=len(topo.engines(src, core)))
+        ops[-1]["after"] = after
+
+    dma("S", ap(B("S0I")), T.s0[:, :], [], [B("S0I")], "d_s0", 2500)
+    dma("A", ap(B("CFI")), T.cf[:, :], [], [B("CFI")], "d_cf", 2500)
+    dma("A", T.Z8I[:, :], T.z0[:, :], [], [B("Z8I")], "d_z0", 2500)
+    dma("S", T.XL0[:, 0:2048], T.xl[:, 0:2048], [], [("XL0", 0, 2048)], "d_xa", 5500)
+    dma("S", T.XL0[:, 2048:4096], T.xl[:, 2048:4096], [], [("XL0", 2048, 4096)], "d_xb", 7500)
+    for c in range(2):
+        for a in range(2):
+            x = ("TT", 256 * c + NC * a, 256 * c + NC * a + NC)
+            dma("A", ap(x), T.t0[:, 256 * a + NC * c:256 * a + NC * c + NC], [], [x], "d_t%d%d" % (c, a), 3500)
+    def iota(o, pat, base, cm):
+        op("G", [lambda: g.iota(ap(o), pat, base, cm)], [], [reg(o)], 130 + 2 * width(o))
+    iota(B("rowI"), [[0, 1]], 0, 1)
+    iota(B("c16"), [[16, 16]], 0, 0)
+    iota(B("colI"), [[1, 128]], 0, 0)
+    AND, SHR = OP.bitwise_and, OP.arith_shift_right
+    ts(B("rrI"), B("rowI"), 15, AND)
+    cp(B("rr"), B("rrI"))
+    ts(B("i16"), B("c16"), B("rr"), OP.add)
+    ts(B("o5a"), B("i16"), 5, OP.mult)
+    ts(B("o5b"), B("o5a"), 255, AND)
+    cp(B("LO"), B("o5b"))
+    ts(B("rgI"), B("rowI"), 4, SHR)
+    cp(B("rg"), B("rgI"))
+    ts(B("cgI"), B("colI"), 4, SHR)
+    cp(B("cg"), B("cgI"))
+    ts(B("r7I"), B("rowI"), 7, AND)
+    cp(B("r7"), B("r7I"))
+    ts(B("q3I"), B("rowI"), 3, SHR)
+    cp(B("q3"), B("q3I"))
+    ts(B("wz"), B("q3"), 0.0, OP.is_equal)
+    ts(B("EXz"), B("cg"), B("r7"), OP.is_equal, B("wz"), OP.mult)
+    cp(B("c8"), ("colI", 0, 8))
+    ts(B("EXs"), B("c8"), B("r7"), OP.is_equal, B("wz"), OP.mult)
+    ts(B("BLKb"), B("cg"), B("rg"), OP.is_equal)
+    ts(B("rp1"), B("rr"), 1.0, OP.add)
+    ts(B("rm8"), B("rr"), -8.0, OP.add)
+    ts(("Z8", 0, 256), ("Z8I", 0, 256), -float(ZC), OP.add)
+    cp(B("CF0"), B("CFI"))
+    gather("V", B("SROT0"), B("S0I"), B("LO"), 1.0, -float(ZC))
+
+    def prep_c(v, q):
+        p = v % 2
+        gather(DQ, B("D%d" % p), B("CF%d" % v), B("LO"), 2.0, 1.0)
+        ts(B("CH%d" % p), B("D%d" % p), 0.5, OP.mult, -0.5, OP.add)
+    prep_c(0, "A")
+    for c in range(2):
+        mm(("pK%d" % c, 0, NC), [(("EXz", 0, 128, "p", 8), ("Z8", c * NC, c * NC + NC, "p", 8))])
+        mm(("pE%d" % c, 128, 136), [(("Z8", c * NC, c * NC + NC, "p", 8), ("EXs", 0, 8, "p", 8))])
+    ts(B("crI"), B("colI"), 15, AND)
+    cp(B("cr"), B("crI"))
+    ts(B("BLKf"), B("cg"), B("rg"), OP.is_equal)
+    ts(B("MA"), B("cr"), 2.0, OP.mult, 21.0, OP.add)
+    tt(B("MMC1"), B("MA"), B("BLKf"), OP.mult)
+    ts(B("wm"), B("rg"), 16.0, OP.mult, B("rr"), OP.add)
+    ts(B("IDb"), B("colI"), B("wm"), OP.is_equal)
+    for c in range(2):
+        ts(B("BM%d" % c), B("cr"), 14.5 - JA[c], OP.is_lt, -16.0, OP.mult)
+        tt(B("BM%d" % c), B("BM%d" % c), B("BLKb"), OP.mult)
+    ms(B("ONE"), 1.0)
+    ts(B("CRW2"), B("cr"), 15.0, OP.is_equal, 524288.0 - 15.0, OP.mult)
+    tt(B("CROW"), B("CRW2"), B("cr"), OP.add)
+    ts(B("G32"), B("c8"), B("rg"), OP.is_equal, 32.0, OP.mult)
+    ts(B("G16"), B("c8"), B("rg"), OP.is_equal, 16.0, OP.mult)
+    ts(B("GM16"), B("c8"), B("rg"), OP.is_equal, -16.0, OP.mult)
+    ts(B("RST"), B("cr"), 0.0, OP.is_equal, 2.0e9, OP.mult)
+    ts(B("RST"), B("RST"), -1.0e9, OP.add)
+    ts(B("IDh"), B("colI"), B("wm"), OP.is_equal)
+    ts(B("wn"), B("q3"), 1.0, OP.is_equal)
+    ts(B("wzn"), B("q3"), 2.0, OP.is_equal, -7.0, OP.mult)
+    tt(B("wn"), B("wn"), B("wzn"), OP.add)
+    tt(B("wzn"), B("wn"), B("wz"), OP.add)
+    ts(B("EXn"), B("cg"), B("r7"), OP.is_equal, B("wn"), OP.mult)
+    ts(B("EXzn"), B("cg"), B("r7"), OP.is_equal, B("wzn"), OP.mult)
+    ts(B("MA"), B("cr"), 2.0, OP.mult, 37.0, OP.add)
+    tt(B("MMC2"), B("MA"), B("BLKf"), OP.mult)
+    ts(B("IDn"), B("IDb"), -1.0, OP.mult)
+    ts(B("rpos"), B("rr"), 0.0, OP.is_gt)
+    ts(B("BLKn"), B("cg"), B("rg"), OP.is_equal, B("rpos"), OP.mult)
+    ts(B("Gn"), B("c8"), B("rg"), OP.is_equal, B("rpos"), OP.mult)
+    ts(B("TRf"), B("cr"), B("rr"), OP.is_ge)
+    tt(B("TRI"), B("TRf"), B("BLKf"), OP.mult)
+    ts(B("G205"), B("c8"), B("rg"), OP.is_equal, 205.0, OP.mult)
+    ms(B("ONEh"), 1.0)
+    ts(B("r16"), B("rr"), 16.0, OP.mult)
+    ts(B("KT"), B("c8"), 256.0, OP.mult, B("r16"), OP.add)
+    ts(B("n205"), B("i16"), 205.0, OP.mult)
+    ms(("SX0", 256, 257), 0.0)
+
+    after = {}
+
+    def send_log(v):
+        dst = T.cores[(rank - v) % n]
+        src = T.cores[(rank + v) % n]
+        a = send(dst, B("CF%d" % v), B("CF0"), "rca%d" % v, "lca%d" % v)
+        recv(B("CF%d" % v), src, "rca%d" % v, 4000, a)
+        for h, x in ((0, "a"), (1, "b")):
+            o = ("XL%d" % v, 2048 * h, 2048 * h + 2048)
+            a = send(dst, o, ("XL0", 2048 * h, 2048 * h + 2048), "rl%s%d" % (x, v), "ll%s%d" % (x, v))
+            recv(o, src, "rl%s%d" % (x, v), 9000 * (1 + h), a)
+
+    send_log(1)
+
+    for m in range(16):
+        x = ("SEL", 128 * m, 128 * m + 128)
+        op("G", [lambda x=x, m=m: g.affine_select(ap(x), ap(B("BLKb")), [[0, 8], [1, 16]], OP.is_equal, 0.0, -m, 0)],
+           [B("BLKb")], [x], 430)
+
+    def lists(t, c, zm, zv, mmc, col, lreg, starts=None):
+        K, P = "pK%d" % c, t % 2
+        i0 = c * NC
+        S, D, C = ("SROT%d" % P, i0, i0 + NC), ("D%d" % P, i0, i0 + NC), ("CH%d" % P, i0, i0 + NC)
+        M, X, XS, CS, LI, LJ, OFF = [B("%s_%d" % (x, c)) for x in ("MASK", "X", "XS", "CS", "LI", "LJ", "OFF")]
+        UZ, OH = ("pT%d" % c, 384, 512), ("pT%d" % c, 256, 384)
+        tt(M, S, (K, zm, zm + NC), OP.is_le)
+        if starts is None:
+            tt(UZ, (K, zv, zv + NC), S, OP.subtract)
+            mm((K, 384, 512), [(B("BLKb"), M)])
+        else:
+            mm((K, 384, 512), [(B("BLKb"), M)])
+            starts()
+            tt(UZ, (K, zv, zv + NC), S, OP.subtract)
+        tt(X, UZ, D, OP.mult)
+        ts(OH, (K, 384, 512), 1.0, OP.max, B("rp1"), OP.is_equal)
+        tt(XS, OH, X, OP.mult)
+        tt(CS, OH, C, OP.mult)
+        mm((K, lreg, lreg + NC), [(B("BLKf"), XS), (B(mmc), CS)])
+        ts(LI, (K, lreg, lreg + NC), B(col), OP.add)
+        ts(LJ, LI, W - 1, AND)
+        cp(OFF, LJ)
+
+    def pick(t, c, dst, parts):
+        a = 0
+        for q, k in parts:
+            gather(q, (dst, 16 * a, 16 * (a + k)), B("XL%d" % t), ("OFF_%d" % c, a, a + k))
+            a += k
+
+    for t in range(NV):
+        P = t % 2
+        last = t == NV - 1
+        for c in range(2):
+            E = "pE%d" % c
+            tag[0] = "L%d" % c
+            zs = (E, 128, 136)
+            ts(B("ZL_%d" % c), zs, -16.0, OP.add, -float(ZC), OP.max)
+            tt(B("DZ_%d" % c), zs, B("ZL_%d" % c), OP.subtract)
+            lists(t, c, 0, 0, "MMC1", "rm8", 256)
+        for c in range(2):
+            tag[0] = "Y%d" % c
+            mm(("pT%d" % c, 0, 256), [(B("IDb"), ("TT", 256 * c, 256 * c + 256))])
+            pick(t, c, "Y_%d" % c, YSPLIT[c])
+        for c in range(2):
+            i0 = c * NC
+            E, Y = "pE%d" % c, "Y_%d" % c
+            er = (E, 0, 128)
+            tag[0] = "M%d" % c
+            mm(er, [(("TT", 256 * c, 256 * c + NC), B("BM%d" % c)), (("ONE", 0, 128, "p", 1), ("CROW", 0, 128, "p", 1))], True, False)
+            for j in range(15 - JA[c]):
+                for a in range(2):
+                    s = (2 * j + a) * NC
+                    tt(("MX_%d" % c, s, s + NC), ("pT%d" % c, 128 * a, 128 * a + 128), (Y, j + a, 16 * NC, 16), OP.max)
+                    mm((E, j, 128, 16), [(("MX_%d" % c, s, s + NC), B("G32")), ((Y, j + a, 16 * NC, 16), B("GM16"))], False, False, er)
+            for b in range(0, JA[c], 2):
+                sl = [(j, a) for j in range(15 - JA[c] + b, min(15, 15 - JA[c] + b + 2)) for a in range(2)]
+                pv = "p%s%d" % ("VK"[b // 2 % 2], c)
+                tag[0] = "A%d" % c
+                for k, (j, a) in enumerate(sl):
+                    mm((pv, NC * k, NC * k + NC), [(B("IDb"), (Y, j + a, 16 * NC, 16)), (B("IDn"), ("TT", 256 * c + NC * a, 256 * c + NC * a + NC))])
+                w, x = NC * len(sl), 2 * b * NC
+                op("A", [lambda c=c, pv=pv, w=w, x=x: g.scalar.activation(T["AX_%d" % c][:, x:x + w], T[pv][:, 0:w], AF.Abs)],
+                   [(pv, 0, w)], [("AX_%d" % c, x, x + w)], w)
+                for k, (j, a) in enumerate(sl):
+                    mm((E, j, 128, 16), [(("AX_%d" % c, x + NC * k, x + NC * k + NC), B("G16"))], False, False, er)
+            tag[0] = "C%d" % c
+            mm(er, [(("TT", 256 * c + NC, 256 * c + 2 * NC), B("BM%d" % c))], False, True)
+            SC, KI, JJ, SM = [B("%s_%d" % (x, c)) for x in ("SC", "KI", "JJ", "SM")]
+            op("V", [lambda c=c, E=E: g.vector.tensor_tensor_scan(T["SC_%d" % c][:, :], T.RST[:, :], T[E][:, 0:128], 1.0e9, OP.max, OP.min)],
+               [er, B("RST")], [SC], 128)
+            key = ("SC_%d" % c, 15, 128, 16)
+            tie = ("SM_%d" % c, 16, 24)
+            cp(KI, key)
+            ts(tie, key, float(16 * TH), OP.is_lt)
+            ts(JJ, KI, 15, AND)
+            tt(B("TD_%d" % c), tie, B("DZ_%d" % c), OP.mult)
+            tt(("SM_%d" % c, 8, 16), JJ, tie, OP.mult)
+            tt(("SM_%d" % c, 0, 8), B("TD_%d" % c), B("ZL_%d" % c), OP.add)
+            mm((E, 128, 256, "p", 24), [(SM, B("IDh"))])
+            cp(("ST_%d" % c, 0, NC), (E, 128, 256, "p", 24))
+            K = "pK%d" % c
+            st = B("ST_%d" % c)
+            for r, x in ((0, "EXz"), (128, "EXzn"), (256, "EXn")):
+                mm((K, r, r + 128), [((x, 0, 128, "p", 24), st)])
+            tag[0] = "R%d" % c
+
+            def starts():
+                tag[0] = "S%d" % c
+                ts(B("GE_%d" % c), (K, 384, 512), B("rp1"), OP.is_le)
+                gd = (E, 256, 384)
+                tt(gd, B("GE_%d" % c), (K, 256, 384), OP.mult)
+                tt(("SX%d" % t, i0, i0 + NC), ("SROT%d" % P, i0, i0 + NC), gd, OP.subtract)
+                tag[0] = "Q%d" % c
+            lists(t, c, 0, 128, "MMC2", "rr", 0, starts)
+        for c in CORD:
+            tag[0] = "S%d" % c
+            lo, hi = c * NC, 257 if c else NC
+            s = send(T.cores[(rank - 1) % n], ("SR%d" % (t + 1), lo, hi), ("SX%d" % t, lo, hi), "rs%d%d" % (t + 1, c), "ls%d%d" % (t + 1, c))
+            recv(("SR%d" % (t + 1), lo, hi), T.cores[(rank + 1) % n], "rs%d%d" % (t + 1, c), RECV, s)
+        if t < 2:
+            send_log(t + 2)
+        if not last:
+            tag[0] = "P"
+            an = ("pE1", 160, 168)
+            mm(an, [(B("ONEh"), ("SM_0", 16, 24)), (B("ONEh"), ("SM_1", 16, 24))])
+            tt(B("AP8"), an, B("G205"), OP.mult)
+            acol = ("SX%d" % (t + 1), 256, 257)
+            op("V", [lambda acol=acol: g.vector.tensor_reduce(ap(acol), T.AP8[:, :], AxisListType.X, OP.add)], [B("AP8")], [acol], 64)
+            ts(B("LA"), B("i16"), acol, OP.add, 5.0, OP.mult)
+            ts(B("LB"), B("LA"), 255, AND)
+            cp(B("LO"), B("LB"))
+            prep_c(t + 1, "A")
+            tt(B("dA"), acol, ("SR%d" % (t + 1), 256, 257), OP.subtract)
+            ts(B("LC"), B("i16"), B("dA"), OP.add)
+            ts(B("LD"), B("LC"), 255, AND)
+            cp(B("LS"), B("LD"))
+            gather(DQ, B("SROT%d" % ((t + 1) % 2)), ("SR%d" % (t + 1), 0, 256), B("LS"))
+        for c in range(2):
+            tag[0] = "V%d" % c
+            pick(t, c, "V_%d" % c, VSPLIT[c])
+        for c in range(2):
+            i0 = c * NC
+            E, K, V, AB, st = "pE%d" % c, "pK%d" % c, "V_%d" % c, "AB_%d" % c, B("ST_%d" % c)
+            for b in range(4):
+                a = 512 * b
+                tag[0] = "D%d" % c
+                vd = ("p%s%d" % ("VT"[b % 2], c), 1, 512)
+                mm(vd, [(B("IDb"), (V, a + 1, a + 512)), (B("IDn"), (V, a, a + 511))])
+                op("A", [lambda AB=AB, a=a, vd=vd: g.scalar.activation(T[AB][:, a + 1:a + 512], ap(vd), AF.Abs)],
+                   [vd], [(AB, a + 1, a + 512)], 512)
+            mm((E, 256, 384), [(("SEL", 128 * m, 128 * m + 128), (AB, m, 16 * NC, 16)) for m in range(2, 16)])
+            tag[0] = "N%d" % c
+            OV, IZ = B("OV_%d" % c), B("IZ_%d" % c)
+            ts(OV, (E, 256, 384), float(TH2), OP.is_gt)
+            mm((E, 384, 512), [(B("TRI"), OV)])
+            ts(IZ, (E, 384, 512), 0.0, OP.is_equal)
+            if last:
+                mm((K, 0, NC, "p", 8), [(("EXs", 0, 8, "p", 24), st), (B("Gn"), IZ)])
+            else:
+                mm((K, 0, NC), [(("EXz", 0, 128, "p", 24), st), (B("BLKn"), IZ)])
+            mm((E, 144, 152), [(("SEL", 128 * p, 128 * p + 128), ("IZ_%d" % c, p, NC, 16)) for p in range(16)] + [(B("IDb"), B("KT"))])
+            if not last:
+                mm((E, 128, 136), [(st, ("EXs", 0, 8, "p", 24)), (IZ, B("Gn"))])
+            for a in range(2):
+                ts(("TO_%d" % c, 8 * a, 8 * a + 8), (E, 144, 152), float(a - 2), OP.add)
+            gather(TQ[c], ("TT", 256 * c, 256 * c + 256), B(V), B("TO_%d" % c))
+            if last:
+                ts(("YZ", i0, i0 + NC), (K, 0, NC, "p", 8), float(ZC), OP.add)
+                for a in range(2):
+                    x = ("TT", 256 * c + NC * a, 256 * c + NC * a + NC)
+                    dma("SA"[a], T.yt[:, 256 * a + i0:256 * a + i0 + NC], ap(x), [x], [], "d_y%s%d" % ("ab"[a], c), 2500)
+    dma("S", T.yz[:, :], T.YZ[:, :], [B("YZ")], [], "d_yz", 2000)
+    ts(B("LC"), B("n205"), ("SR4", 256, 257), OP.subtract)
+    ts(B("LD"), B("LC"), 255, AND)
+    cp(B("LS"), B("LD"))
+    gather("V", B("YSO"), ("SR4", 0, 256), B("LS"), 1.0, float(ZC))
+    dma("S", T.ys[:, :], T.YSO[:, :], [B("YSO")], [], "d_ys", 2500)
+    return ops
+
+
+def link(ops):
+    hist = {}
+    for k, o in enumerate(ops):
+        deps = {}
+
+        def add(x, hard):
+            deps[x] = deps.get(x, False) or hard
+        if "after" in o:
+            add(o["after"], False)
+        acc = [(r, False) for r in o["r"]] + [(w, True) for w in o["w"]]
+        for (b, lo, hi), wr in acc:
+            ps = SCRATCH[b][0] == "psum"
+            for (x, l2, h2, w2) in hist.get(b, ()):
+                if x == k:
+                    continue
+                same = ops[x]["q"] == o["q"]
+                if ps and (not same):
+                    add(x, True)
+                elif ps and o["q"] == "P":
+                    add(x, False)
+                elif (wr or w2) and lo < h2 and l2 < hi:
+                    add(x, True)
+        for (b, lo, hi), wr in acc:
+            h = hist.setdefault(b, [])
+            ps = SCRATCH[b][0] == "psum"
+            if wr and not ps:
+                h[:] = [y for y in h if not (lo <= y[1] and y[2] <= hi and y[0] != k)]
+            if ps:
+                h[:] = [y for y in h if ops[y[0]]["q"] != o["q"] or y[0] == k or (o["q"] != "P" and not (wr and lo <= y[1] and y[2] <= hi))] if o["q"] == "P" or wr else h
+            h.append((k, lo, hi, wr))
+        o["deps"] = deps
+
+
+def order(ops):
+    n = len(ops)
+    succ = [[] for _ in range(n)]
+    need = [0] * n
+    for k, o in enumerate(ops):
+        for x in o["deps"]:
+            succ[x].append(k)
+            need[k] += 1
+    way = [0.0] * n
+    for k in range(n - 1, -1, -1):
+        way[k] = ops[k]["cost"] + SYNCNS + max([way[s] for s in succ[k]] + [0.0])
+    for k, o in enumerate(ops):
+        way[k] += BI.get(o["tag"], 0)
+    prev = {}
+    for k, o in enumerate(ops):
+        if o["kind"] in ("dma", "send") or o["q"] == "G":
+            if o["q"] in prev:
+                succ[prev[o["q"]]].append(k)
+                need[k] += 1
+            prev[o["q"]] = k
+    ready_at = [0.0] * n
+    ready = {}
+    free = {}
+    seq = []
+
+    def push(k):
+        ready.setdefault(ops[k]["q"], []).append(k)
+    for k in range(n):
+        if need[k] == 0:
+            push(k)
+    while any(ready.values()):
+        best = None
+        for q, l in ready.items():
+            if not l:
+                continue
+            f = free.get(q, 0.0) if q != "R" else 0.0
+            t0 = max(f, min(ready_at[k] for k in l))
+            k = min((k for k in l if ready_at[k] <= t0 + 1e-6), key=lambda k: (-way[k], k))
+            if best is None or t0 < best[0]:
+                best = (t0, q, k)
+        t0, q, k = best
+        ready[q].remove(k)
+        o = ops[k]
+        busy = {"dma": 60.0, "recv": 0.0, "send": o["cost"]}.get(o["kind"], o["cost"])
+        free[q] = t0 + busy
+        o["t0"] = t0
+        end = t0 + o["cost"] + SYNCNS
+        seq.append(k)
+        for s in succ[k]:
+            e = t0 + busy if (k not in ops[s]["deps"] or ops[s]["q"] == q and not ops[s]["deps"][k]) else end
+            ready_at[s] = max(ready_at[s], e)
+            need[s] -= 1
+            if need[s] == 0:
+                push(s)
+    return seq
+
+
+def emit(g, T, ops, seq):
+    queue = {"V": g.vector, "A": g.scalar, "P": g.tensor, "G": g, "S": g.sync}
+    total = {"V": 0, "A": 0, "P": 0, "G": 0}
+    know = {q: {} for q in queue}
+    waited = {}
+    issued = []
+    for k in seq:
+        o = ops[k]
+        q = o["q"]
+        if o["kind"] == "recv":
+            o["done"] = (o["sem"], o["cnt"])
+            o["clock"] = {}
+            issued.append(o["done"])
+            continue
+        eng = queue[q]
+        for x in sorted(o["deps"], reverse=True):
+            if not o["deps"][x]:
+                continue
+            d = ops[x]
+            s, v = d["done"]
+            if know[q].get(s, 0) >= v:
+                continue
+            eng.wait_ge(T.sem[s], v)
+            waited[s] = max(waited.get(s, 0), v)
+            know[q][s] = v
+            for s2, v2 in d["clock"].items():
+                if know[q].get(s2, 0) < v2:
+                    know[q][s2] = v2
+        if o["kind"] == "c":
+            for f in o["fns"]:
+                f().then_inc(T.sem["s" + q], 1)
+            total[q] += len(o["fns"])
+            o["done"] = ("s" + q, total[q])
+        elif o["kind"] == "dma":
+            for f in o["fns"]:
+                f().then_inc(T.sem[o["sem"]], 16)
+            o["done"] = (o["sem"], 16)
+        else:
+            for f in o["fns"]:
+                f()
+            o["done"] = (o["sem"], o["cnt"])
+        o["clock"] = dict(know[q])
+        if o["kind"] != "c":
+            issued.append(o["done"])
+    for q in total:
+        if total[q]:
+            issued.append(("s" + q, total[q]))
+    for s, v in issued:
+        if know["G"].get(s, 0) < v:
+            g.wait_ge(T.sem[s], v)
+
+
+def rank_program(g, core, T, topo):
+    if T.rank_of(core) is None:
+        return
+    ops = plan(g, core, T, topo)
+    link(ops)
+    emit(g, T, ops, order(ops))

@@ -7,14 +7,14 @@ OP = AluOpType
 AF = ActivationFunctionType
 NV, W, ZC, TH, TH2 = 4, 4096, 1536, 1082, 820
 NC = 128
-SYNCNS = 70
+SYNCNS = 100
 PE_NS = 0.5
-JA = (4, 4)
-YSPLIT = [[("V", 32), ("A", 96)], [("A", 128)]]
-VSPLIT = [[("A", 128)], [("V", 48), ("A", 80)]]
+JA = (8, 4)
+YSPLIT = [[("V", 64), ("A", 64)], [("A", 128)]]
+VSPLIT = [[("V", 32), ("A", 32), ("V", 32), ("A", 32)]] * 2
 TQ = ("V", "A")
-DQ = "A"
-BI = {'M1': -7800, 'S0': -3315, 'L1': -6658, 'M0': -4480, 'N1': -6905, 'D1': -5589, 'Q0': -3380, 'A1': -8198, 'Q1': -4886, 'N0': 12695, 'C1': 992, 'S1': -2446, 'R0': -1246, 'A0': -1072, 'V0': -6089, 'Y1': 4200, 'L0': 6209, 'Y0': -679, 'P': -1558, 'D0': 281, 'V1': -1114, 'C0': -2842}
+DQ = "V"
+BI = {'M0': -19957, 'S0': 8812, 'Q0': 8916, 'A0': -13949, 'V1': -3468, 'M1': -4459, 'C0': -1044, 'N0': 789, 'D1': -6115, 'V0': -5027, 'C1': -327, 'R0': -3667, 'L1': -1914, 'D0': 5816, 'P': 922, 'A1': 9610, 'R1': 6757, 'Y1': 901}
 CORD = (1, 0)
 RECV = 2500
 GN = 1.56
@@ -34,8 +34,7 @@ for _v in range(4):
 for _n, _c, _d in (("CFI", 256, "int32"), ("S0I", 256, "int32"), ("TT", 512, "bfloat16"), ("YSO", 256, "float32"),
                    ("SROT0", 256, "float32"), ("SROT1", 256, "float32"), ("D0", 256, "float32"), ("D1", 256, "float32"),
                    ("CH0", 256, "float16"), ("CH1", 256, "float16"),
-                   ("colI", 128, "int32"), ("cgI", 128, "int32"), ("crI", 128, "int32"),
-                   ("c8", 8, "float32"), ("BLKf", 128, "float32"), ("SEL", 2048, "bfloat16"), ("IDh", 128, "float16"),
+                   ("BLKf", 128, "float32"), ("SEL", 2048, "bfloat16"), ("IDh", 128, "float16"),
                    ("MMC1", 128, "float16"), ("MMC2", 128, "float16"),
                    ("G32", 8, "bfloat16"), ("GM16", 8, "bfloat16"), ("G16", 8, "bfloat16"), ("Gn", 8, "bfloat16"), ("G205", 8, "float32"),
                    ("RST", 128, "float32"), ("ONE", 128, "bfloat16"), ("ONEh", 128, "float16"), ("CROW", 128, "bfloat16"),
@@ -45,7 +44,7 @@ for _n, _c, _d in (("CFI", 256, "int32"), ("S0I", 256, "int32"), ("TT", 512, "bf
     _b(_n, _c, _d)
 VIRT = {}
 for _p, _c, _d, _l in (("PF", 1, "float32", "rg rr r7 q3 rp1 rm8 rpos wz wn wm wzn r16 dA"), ("PI", 1, "int32", "rowI rgI rrI r7I q3I"),
-                       ("PJ", 16, "int32", "c16 i16 n205 o5a o5b LA LB LC LD"), ("PG", 128, "float32", "cg cr TRf MA CRW2"),
+                       ("PJ", 16, "int32", "c16 i16 n205 o5a o5b LA LB LC LD"), ("PG", 128, "float32", "cg cr colF TRf MA MB RS0 CRW2"),
                        ("PB", 128, "bfloat16", "BLKb BLKn BM0 BM1 TRI IDb IDn")):
     for _k, _n in enumerate(_l.split()):
         VIRT[_n] = (_p, _k * _c, _c)
@@ -177,10 +176,20 @@ def plan(g, core, T, topo):
             x = ("TT", 256 * c + NC * a, 256 * c + NC * a + NC)
             dma("A", ap(x), T.t0[:, 256 * a + NC * c:256 * a + NC * c + NC], [], [x], "d_t%d%d" % (c, a), 3500)
     def iota(o, pat, base, cm):
-        op("G", [lambda: g.iota(ap(o), pat, base, cm)], [], [reg(o)], 130 + 2 * width(o))
+        if SCRATCH[o[0]][2] == "int32":
+            f = [lambda: g.iota(ap(o), pat, base, cm)]
+        else:
+            f = [lambda: g.iota(ap(o), pat, base, cm, allow_small_or_imprecise_dtypes=True)]
+        op("G", f, [], [reg(o)], 130 + 2 * width(o))
+
+    def act(o, a, bias, scale):
+        op("A", [lambda: g.scalar.activation(ap(o), ap(a), AF.Identity, bias=bias, scale=scale)], [reg(a)], [reg(o)], max(64, width(o)))
     iota(B("rowI"), [[0, 1]], 0, 1)
     iota(B("c16"), [[16, 16]], 0, 0)
-    iota(B("colI"), [[1, 128]], 0, 0)
+    iota(B("cg"), [[1, 8], [0, 16]], 0, 0)
+    iota(B("cr"), [[0, 8], [1, 16]], 0, 0)
+    iota(B("colF"), [[1, 128]], 0, 0)
+    iota(B("wm"), [[0, 1]], 0, 1)
     AND, SHR = OP.bitwise_and, OP.arith_shift_right
     ts(B("rrI"), B("rowI"), 15, AND)
     cp(B("rr"), B("rrI"))
@@ -190,16 +199,14 @@ def plan(g, core, T, topo):
     cp(B("LO"), B("o5b"))
     ts(B("rgI"), B("rowI"), 4, SHR)
     cp(B("rg"), B("rgI"))
-    ts(B("cgI"), B("colI"), 4, SHR)
-    cp(B("cg"), B("cgI"))
     ts(B("r7I"), B("rowI"), 7, AND)
     cp(B("r7"), B("r7I"))
     ts(B("q3I"), B("rowI"), 3, SHR)
     cp(B("q3"), B("q3I"))
     ts(B("wz"), B("q3"), 0.0, OP.is_equal)
     ts(B("EXz"), B("cg"), B("r7"), OP.is_equal, B("wz"), OP.mult)
-    cp(B("c8"), ("colI", 0, 8))
-    ts(B("EXs"), B("c8"), B("r7"), OP.is_equal, B("wz"), OP.mult)
+    c8 = (B("colF")[0], B("colF")[1], B("colF")[1] + 8)
+    ts(B("EXs"), c8, B("r7"), OP.is_equal, B("wz"), OP.mult)
     ts(B("BLKb"), B("cg"), B("rg"), OP.is_equal)
     ts(B("rp1"), B("rr"), 1.0, OP.add)
     ts(B("rm8"), B("rr"), -8.0, OP.add)
@@ -215,43 +222,40 @@ def plan(g, core, T, topo):
     for c in range(2):
         mm(("pK%d" % c, 0, NC), [(("EXz", 0, 128, "p", 8), ("Z8", c * NC, c * NC + NC, "p", 8))])
         mm(("pE%d" % c, 128, 136), [(("Z8", c * NC, c * NC + NC, "p", 8), ("EXs", 0, 8, "p", 8))])
-    ts(B("crI"), B("colI"), 15, AND)
-    cp(B("cr"), B("crI"))
     ts(B("BLKf"), B("cg"), B("rg"), OP.is_equal)
-    ts(B("MA"), B("cr"), 2.0, OP.mult, 21.0, OP.add)
+    act(B("MA"), B("cr"), 21.0, 2.0)
     tt(B("MMC1"), B("MA"), B("BLKf"), OP.mult)
-    ts(B("wm"), B("rg"), 16.0, OP.mult, B("rr"), OP.add)
-    ts(B("IDb"), B("colI"), B("wm"), OP.is_equal)
+    ts(B("IDb"), B("colF"), B("wm"), OP.is_equal)
     for c in range(2):
         ts(B("BM%d" % c), B("cr"), 14.5 - JA[c], OP.is_lt, -16.0, OP.mult)
         tt(B("BM%d" % c), B("BM%d" % c), B("BLKb"), OP.mult)
     ms(B("ONE"), 1.0)
     ts(B("CRW2"), B("cr"), 15.0, OP.is_equal, 524288.0 - 15.0, OP.mult)
     tt(B("CROW"), B("CRW2"), B("cr"), OP.add)
-    ts(B("G32"), B("c8"), B("rg"), OP.is_equal, 32.0, OP.mult)
-    ts(B("G16"), B("c8"), B("rg"), OP.is_equal, 16.0, OP.mult)
-    ts(B("GM16"), B("c8"), B("rg"), OP.is_equal, -16.0, OP.mult)
-    ts(B("RST"), B("cr"), 0.0, OP.is_equal, 2.0e9, OP.mult)
-    ts(B("RST"), B("RST"), -1.0e9, OP.add)
-    ts(B("IDh"), B("colI"), B("wm"), OP.is_equal)
+    ts(B("G32"), c8, B("rg"), OP.is_equal, 32.0, OP.mult)
+    act(B("G16"), B("G32"), 0.0, 0.5)
+    act(B("GM16"), B("G32"), 0.0, -0.5)
+    ts(B("RS0"), B("cr"), 0.0, OP.is_equal)
+    act(B("RST"), B("RS0"), -1.0e9, 2.0e9)
+    ts(B("IDh"), B("colF"), B("wm"), OP.is_equal)
     ts(B("wn"), B("q3"), 1.0, OP.is_equal)
     ts(B("wzn"), B("q3"), 2.0, OP.is_equal, -7.0, OP.mult)
     tt(B("wn"), B("wn"), B("wzn"), OP.add)
     tt(B("wzn"), B("wn"), B("wz"), OP.add)
     ts(B("EXn"), B("cg"), B("r7"), OP.is_equal, B("wn"), OP.mult)
     ts(B("EXzn"), B("cg"), B("r7"), OP.is_equal, B("wzn"), OP.mult)
-    ts(B("MA"), B("cr"), 2.0, OP.mult, 37.0, OP.add)
-    tt(B("MMC2"), B("MA"), B("BLKf"), OP.mult)
-    ts(B("IDn"), B("IDb"), -1.0, OP.mult)
+    act(B("MB"), B("cr"), 37.0, 2.0)
+    tt(B("MMC2"), B("MB"), B("BLKf"), OP.mult)
+    act(B("IDn"), B("IDb"), 0.0, -1.0)
     ts(B("rpos"), B("rr"), 0.0, OP.is_gt)
     ts(B("BLKn"), B("cg"), B("rg"), OP.is_equal, B("rpos"), OP.mult)
-    ts(B("Gn"), B("c8"), B("rg"), OP.is_equal, B("rpos"), OP.mult)
+    ts(B("Gn"), c8, B("rg"), OP.is_equal, B("rpos"), OP.mult)
     ts(B("TRf"), B("cr"), B("rr"), OP.is_ge)
     tt(B("TRI"), B("TRf"), B("BLKf"), OP.mult)
-    ts(B("G205"), B("c8"), B("rg"), OP.is_equal, 205.0, OP.mult)
+    ts(B("G205"), c8, B("rg"), OP.is_equal, 205.0, OP.mult)
     ms(B("ONEh"), 1.0)
     ts(B("r16"), B("rr"), 16.0, OP.mult)
-    ts(B("KT"), B("c8"), 256.0, OP.mult, B("r16"), OP.add)
+    ts(B("KT"), c8, 256.0, OP.mult, B("r16"), OP.add)
     ts(B("n205"), B("i16"), 205.0, OP.mult)
     ms(("SX0", 256, 257), 0.0)
 
@@ -404,7 +408,8 @@ def plan(g, core, T, topo):
                 mm(vd, [(B("IDb"), (V, a + 1, a + 512)), (B("IDn"), (V, a, a + 511))])
                 op("A", [lambda AB=AB, a=a, vd=vd: g.scalar.activation(T[AB][:, a + 1:a + 512], ap(vd), AF.Abs)],
                    [vd], [(AB, a + 1, a + 512)], 512)
-            mm((E, 256, 384), [(("SEL", 128 * m, 128 * m + 128), (AB, m, 16 * NC, 16)) for m in range(2, 16)])
+                if b % 2:
+                    mm((E, 224 + 32 * b, 288 + 32 * b), [(("SEL", 128 * m, 128 * m + 128), (AB, 512 * b - 512 + m, 512 * b + 512, 16)) for m in range(2, 16)])
             tag[0] = "N%d" % c
             OV, IZ = B("OV_%d" % c), B("IZ_%d" % c)
             ts(OV, (E, 256, 384), float(TH2), OP.is_gt)

import numpy as np
import comms_topo
from concourse.bass import DstId, RemoteDMATransfer
from concourse.mybir import dt, AluOpType, AxisListType, ActivationFunctionType

OP = AluOpType
AF = ActivationFunctionType
NV, W, ZC, TH, TH2 = 4, 4096, 1536, 1082, 820
NC = 128
SYNCNS = 100
PE_NS = 0.5
JA = (8, 4)
YSPLIT = [[("V", 64), ("A", 64)], [("A", 128)]]
VSPLIT = [[("V", 32), ("A", 32), ("V", 32), ("A", 32)]] * 2
TQ = ("V", "A")
DQ = "V"
BI = {'M0': -19957, 'S0': 8812, 'Q0': 8916, 'A0': -13949, 'V1': -3468, 'M1': -4459, 'C0': -1044, 'N0': 789, 'D1': -6115, 'V0': -5027, 'C1': -327, 'R0': -3667, 'L1': -1914, 'D0': 5816, 'P': 922, 'A1': 9610, 'R1': 6757, 'Y1': 901}
CORD = (1, 0)
RECV = 2500
GN = 1.56

SCRATCH = {}


def _b(name, cols, dtype, where="sbuf", rows=128):
    SCRATCH[name] = (where, [rows, cols], dtype)


for _v in range(4):
    _b("XL%d" % _v, W, "bfloat16")
    _b("CF%d" % _v, 256, "float32")
    _b("SX%d" % _v, 257, "float32")
    _b("SR%d" % (_v + 1), 257, "float32")
for _n, _c, _d in (("CFI", 256, "int32"), ("S0I", 256, "int32"), ("TT", 512, "bfloat16"), ("YSO", 256, "float32"),
                   ("SROT0", 256, "float32"), ("SROT1", 256, "float32"), ("D0", 256, "float32"), ("D1", 256, "float32"),
                   ("CH0", 256, "float16"), ("CH1", 256, "float16"),
                   ("BLKf", 128, "float32"), ("SEL", 2048, "bfloat16"), ("IDh", 128, "float16"),
                   ("MMC1", 128, "float16"), ("MMC2", 128, "float16"),
                   ("G32", 8, "bfloat16"), ("GM16", 8, "bfloat16"), ("G16", 8, "bfloat16"), ("Gn", 8, "bfloat16"), ("G205", 8, "float32"),
                   ("RST", 128, "float32"), ("ONE", 128, "bfloat16"), ("ONEh", 128, "float16"), ("CROW", 128, "bfloat16"),
                   ("KT", 8, "bfloat16"),
                   ("EXz", 128, "float16"), ("EXn", 128, "float16"), ("EXzn", 128, "float16"), ("EXs", 8, "float16"),
                   ("AP8", 8, "float32"), ("LO", 16, "uint16"), ("LS", 16, "uint16")):
    _b(_n, _c, _d)
VIRT = {}
for _p, _c, _d, _l in (("PF", 1, "float32", "rg rr r7 q3 rp1 rm8 rpos wz wn wm wzn r16 dA"), ("PI", 1, "int32", "rowI rgI rrI r7I q3I"),
                       ("PJ", 16, "int32", "c16 i16 n205 o5a o5b LA LB LC LD"), ("PG", 128, "float32", "cg cr colF TRf MA MB RS0 CRW2"),
                       ("PB", 128, "bfloat16", "BLKb BLKn BM0 BM1 TRI IDb IDn")):
    for _k, _n in enumerate(_l.split()):
        VIRT[_n] = (_p, _k * _c, _c)
    _b(_p, _c * len(_l.split()), _d)
_b("Z8I", 256, "int32", rows=8)
_b("Z8", 256, "float16", rows=8)
_b("YZ", 256, "float32", rows=8)
for _k in range(2):
    for _n, _c, _d in (("MASK", NC, "bfloat16"), ("X", NC, "float32"), ("XS", NC, "float32"), ("CS", NC, "float16"),
                       ("LI", NC, "int32"), ("LJ", NC, "int32"), ("OFF", NC, "uint16"), ("Y", 16 * NC, "bfloat16"),
                       ("V", 16 * NC, "bfloat16"), ("MX", 30 * NC, "bfloat16"), ("AX", max(1, 2 * max(JA)) * NC, "bfloat16"), ("SC", 128, "float32"), ("KI", 8, "int32"),
                       ("JJ", 8, "int32"), ("DZ", 8, "float32"), ("ZL", 8, "float32"), ("TD", 8, "float32"),
                       ("SM", 24, "float16"), ("GE", NC, "float32"), ("AB", 16 * NC, "bfloat16"),
                       ("OV", NC, "bfloat16"), ("IZ", NC, "bfloat16"), ("TO", 16, "uint16")):
        _b("%s_%d" % (_n, _k), _c, _d)
    _b("ST_%d" % _k, NC, "float16", rows=24)
    for _n in ("K", "T", "E", "V"):
        _b("p%s%d" % (_n, _k), 512, "float32", where="psum")

SEMAPHORES = ["sV", "sA", "sP", "sG"]
SEMAPHORES += ["d_" + n for n in ("s0", "cf", "z0", "t00", "t01", "t10", "t11", "xa", "xb", "ys", "yz", "ya0", "ya1", "yb0", "yb1")]
for _v in range(1, 4):
    SEMAPHORES += ["%s%d" % (n, _v) for n in ("rca", "rla", "rlb", "lca", "lla", "llb")]
for _v in range(1, 5):
    SEMAPHORES += ["%s%d%d" % (n, _v, c) for n in ("rs", "ls") for c in range(2)]


class _Plan(dict):
    pass


def plan(g, core, T, topo):
    rank = T.rank_of(core)
    n = len(T.cores)
    ops = []
    tag = ["c"]

    def B(name):
        if name in VIRT:
            p, lo, c = VIRT[name]
            return (p, lo, lo + c)
        return (name, 0, SCRATCH[name][1][1])

    def op(q, fns, reads, writes, cost, kind="c", sem=None, cnt=0):
        ops.append(dict(tag=tag[0], q=q, fns=fns, r=reads, w=writes, cost=cost, kind=kind, sem=sem, cnt=cnt))
        return len(ops) - 1

    def ap(x):
        if len(x) == 3:
            return T[x[0]][:, x[1]:x[2]]
        if x[3] == "p":
            return T[x[0]][0:x[4], x[1]:x[2]]
        return T[x[0]][:, x[1]:x[2]:x[3]]

    def width(x):
        if len(x) > 3 and x[3] != "p":
            return -(-(x[2] - x[1]) // x[3])
        return x[2] - x[1]

    def psum(x):
        return SCRATCH[x[0]][0] == "psum"

    def reg(x):
        return (x[0], x[1], x[2])

    def tt(o, a, b, alu):
        c = width(o) * (1 if psum(a) or psum(b) else 2)
        op("V", [lambda: g.vector.tensor_tensor(ap(o), ap(a), ap(b), alu)], [reg(a), reg(b)], [reg(o)], max(64, c))

    def sc(x):
        return ap(x) if isinstance(x, tuple) else x

    def ts(o, a, s1, op0, s2=None, op1=None):
        rd = [reg(a)] + [reg(s) for s in (s1, s2) if isinstance(s, tuple)]
        if op1 is None:
            f = [lambda: g.vector.tensor_scalar(ap(o), ap(a), sc(s1), None, op0)]
        else:
            f = [lambda: g.vector.tensor_scalar(ap(o), ap(a), sc(s1), sc(s2), op0, op1)]
        op("V", f, rd, [reg(o)], max(64, width(o)))

    def cp(o, a):
        op("V", [lambda: g.vector.tensor_copy(ap(o), ap(a))], [reg(a)], [reg(o)], max(64, width(o)))

    def ms(o, val):
        op("V", [lambda: g.vector.memset(ap(o), val)], [], [reg(o)], max(64, width(o)))

    def gather(q, o, win, off, scale=1.0, bias=0.0):
        cost = 60 + GN * width(o)
        if q == "V":
            f = lambda: g.vector.tensor_copy(ap(o), ap(win).indirect(ap(off)))
            if scale != 1.0 or bias != 0.0:
                f = lambda: g.vector.tensor_scalar(ap(o), ap(win).indirect(ap(off)), scale, bias, OP.mult, OP.add)
        else:
            f = lambda: g.scalar.activation(ap(o), ap(win).indirect(ap(off)), AF.Copy)
            if scale != 1.0 or bias != 0.0:
                f = lambda: g.scalar.activation(ap(o), ap(win).indirect(ap(off)), AF.Identity, bias=bias, scale=scale)
        op(q, [f], [reg(win), reg(off)], [reg(o)], cost)

    def mm(o, pairs, start=True, stop=True, wreg=None):
        fns, rd, cost = [], [], 0
        for k, (l, r) in enumerate(pairs):
            fns.append(lambda l=l, r=r, k=k: g.tensor.matmul(ap(o), ap(l), ap(r), start and k == 0, stop and k == len(pairs) - 1))
            rd += [reg(l), reg(r)]
            cost += max(min(64, width(l)), width(r)) * (4 if SCRATCH[l[0]][2] == "float32" else 1) * PE_NS
        op("P", fns, rd, [wreg or reg(o)], cost)

    def dma(q, o, a, rd, wr, sem, cost):
        eng = g.sync if q == "S" else g.scalar
        op(q, [lambda: eng.dma_start(o, a)], rd, wr, cost, kind="dma", sem=sem)

    def send(dst, out, src, rs, ls):
        rid, pid = topo.addr(dst, core)
        m = topo.mask(core, dst)
        op("G", [lambda: g.remote_dma(ap(out), ap(src), T.sem[rs], T.sem[ls], pid, rid, m)], [reg(src)], [], 1000,
           kind="send", sem=ls, cnt=len(topo.engines(core, dst)))
        return len(ops) - 1

    def recv(o, src, rs, cost, after):
        op("R", [], [], [reg(o)], cost, kind="recv", sem=rs, cnt=len(topo.engines(src, core)))
        ops[-1]["after"] = after

    dma("S", ap(B("S0I")), T.s0[:, :], [], [B("S0I")], "d_s0", 2500)
    dma("A", ap(B("CFI")), T.cf[:, :], [], [B("CFI")], "d_cf", 2500)
    dma("A", T.Z8I[:, :], T.z0[:, :], [], [B("Z8I")], "d_z0", 2500)
    dma("S", T.XL0[:, 0:2048], T.xl[:, 0:2048], [], [("XL0", 0, 2048)], "d_xa", 5500)
    dma("S", T.XL0[:, 2048:4096], T.xl[:, 2048:4096], [], [("XL0", 2048, 4096)], "d_xb", 7500)
    for c in range(2):
        for a in range(2):
            x = ("TT", 256 * c + NC * a, 256 * c + NC * a + NC)
            dma("A", ap(x), T.t0[:, 256 * a + NC * c:256 * a + NC * c + NC], [], [x], "d_t%d%d" % (c, a), 3500)
    def iota(o, pat, base, cm):
        if SCRATCH[o[0]][2] == "int32":
            f = [lambda: g.iota(ap(o), pat, base, cm)]
        else:
            f = [lambda: g.iota(ap(o), pat, base, cm, allow_small_or_imprecise_dtypes=True)]
        op("G", f, [], [reg(o)], 130 + 2 * width(o))

    def act(o, a, bias, scale):
        op("A", [lambda: g.scalar.activation(ap(o), ap(a), AF.Identity, bias=bias, scale=scale)], [reg(a)], [reg(o)], max(64, width(o)))
    iota(B("rowI"), [[0, 1]], 0, 1)
    iota(B("c16"), [[16, 16]], 0, 0)
    iota(B("cg"), [[1, 8], [0, 16]], 0, 0)
    iota(B("cr"), [[0, 8], [1, 16]], 0, 0)
    iota(B("colF"), [[1, 128]], 0, 0)
    iota(B("wm"), [[0, 1]], 0, 1)
    AND, SHR = OP.bitwise_and, OP.arith_shift_right
    ts(B("rrI"), B("rowI"), 15, AND)
    cp(B("rr"), B("rrI"))
    ts(B("i16"), B("c16"), B("rr"), OP.add)
    ts(B("o5a"), B("i16"), 5, OP.mult)
    ts(B("o5b"), B("o5a"), 255, AND)
    cp(B("LO"), B("o5b"))
    ts(B("rgI"), B("rowI"), 4, SHR)
    cp(B("rg"), B("rgI"))
    ts(B("r7I"), B("rowI"), 7, AND)
    cp(B("r7"), B("r7I"))
    ts(B("q3I"), B("rowI"), 3, SHR)
    cp(B("q3"), B("q3I"))
    ts(B("wz"), B("q3"), 0.0, OP.is_equal)
    ts(B("EXz"), B("cg"), B("r7"), OP.is_equal, B("wz"), OP.mult)
    c8 = (B("colF")[0], B("colF")[1], B("colF")[1] + 8)
    ts(B("EXs"), c8, B("r7"), OP.is_equal, B("wz"), OP.mult)
    ts(B("BLKb"), B("cg"), B("rg"), OP.is_equal)
    ts(B("rp1"), B("rr"), 1.0, OP.add)
    ts(B("rm8"), B("rr"), -8.0, OP.add)
    ts(("Z8", 0, 256), ("Z8I", 0, 256), -float(ZC), OP.add)
    cp(B("CF0"), B("CFI"))
    gather("V", B("SROT0"), B("S0I"), B("LO"), 1.0, -float(ZC))

    def prep_c(v, q):
        p = v % 2
        gather(DQ, B("D%d" % p), B("CF%d" % v), B("LO"), 2.0, 1.0)
        ts(B("CH%d" % p), B("D%d" % p), 0.5, OP.mult, -0.5, OP.add)
    prep_c(0, "A")
    for c in range(2):
        mm(("pK%d" % c, 0, NC), [(("EXz", 0, 128, "p", 8), ("Z8", c * NC, c * NC + NC, "p", 8))])
        mm(("pE%d" % c, 128, 136), [(("Z8", c * NC, c * NC + NC, "p", 8), ("EXs", 0, 8, "p", 8))])
    ts(B("BLKf"), B("cg"), B("rg"), OP.is_equal)
    act(B("MA"), B("cr"), 21.0, 2.0)
    tt(B("MMC1"), B("MA"), B("BLKf"), OP.mult)
    ts(B("IDb"), B("colF"), B("wm"), OP.is_equal)
    for c in range(2):
        ts(B("BM%d" % c), B("cr"), 14.5 - JA[c], OP.is_lt, -16.0, OP.mult)
        tt(B("BM%d" % c), B("BM%d" % c), B("BLKb"), OP.mult)
    ms(B("ONE"), 1.0)
    ts(B("CRW2"), B("cr"), 15.0, OP.is_equal, 524288.0 - 15.0, OP.mult)
    tt(B("CROW"), B("CRW2"), B("cr"), OP.add)
    ts(B("G32"), c8, B("rg"), OP.is_equal, 32.0, OP.mult)
    act(B("G16"), B("G32"), 0.0, 0.5)
    act(B("GM16"), B("G32"), 0.0, -0.5)
    ts(B("RS0"), B("cr"), 0.0, OP.is_equal)
    act(B("RST"), B("RS0"), -1.0e9, 2.0e9)
    ts(B("IDh"), B("colF"), B("wm"), OP.is_equal)
    ts(B("wn"), B("q3"), 1.0, OP.is_equal)
    ts(B("wzn"), B("q3"), 2.0, OP.is_equal, -7.0, OP.mult)
    tt(B("wn"), B("wn"), B("wzn"), OP.add)
    tt(B("wzn"), B("wn"), B("wz"), OP.add)
    ts(B("EXn"), B("cg"), B("r7"), OP.is_equal, B("wn"), OP.mult)
    ts(B("EXzn"), B("cg"), B("r7"), OP.is_equal, B("wzn"), OP.mult)
    act(B("MB"), B("cr"), 37.0, 2.0)
    tt(B("MMC2"), B("MB"), B("BLKf"), OP.mult)
    act(B("IDn"), B("IDb"), 0.0, -1.0)
    ts(B("rpos"), B("rr"), 0.0, OP.is_gt)
    ts(B("BLKn"), B("cg"), B("rg"), OP.is_equal, B("rpos"), OP.mult)
    ts(B("Gn"), c8, B("rg"), OP.is_equal, B("rpos"), OP.mult)
    ts(B("TRf"), B("cr"), B("rr"), OP.is_ge)
    tt(B("TRI"), B("TRf"), B("BLKf"), OP.mult)
    ts(B("G205"), c8, B("rg"), OP.is_equal, 205.0, OP.mult)
    ms(B("ONEh"), 1.0)
    ts(B("r16"), B("rr"), 16.0, OP.mult)
    ts(B("KT"), c8, 256.0, OP.mult, B("r16"), OP.add)
    ts(B("n205"), B("i16"), 205.0, OP.mult)
    ms(("SX0", 256, 257), 0.0)

    after = {}

    def send_log(v):
        dst = T.cores[(rank - v) % n]
        src = T.cores[(rank + v) % n]
        a = send(dst, B("CF%d" % v), B("CF0"), "rca%d" % v, "lca%d" % v)
        recv(B("CF%d" % v), src, "rca%d" % v, 4000, a)
        for h, x in ((0, "a"), (1, "b")):
            o = ("XL%d" % v, 2048 * h, 2048 * h + 2048)
            a = send(dst, o, ("XL0", 2048 * h, 2048 * h + 2048), "rl%s%d" % (x, v), "ll%s%d" % (x, v))
            recv(o, src, "rl%s%d" % (x, v), 9000 * (1 + h), a)

    send_log(1)

    for m in range(16):
        x = ("SEL", 128 * m, 128 * m + 128)
        op("G", [lambda x=x, m=m: g.affine_select(ap(x), ap(B("BLKb")), [[0, 8], [1, 16]], OP.is_equal, 0.0, -m, 0)],
           [B("BLKb")], [x], 430)

    def lists(t, c, zm, zv, mmc, col, lreg, starts=None):
        K, P = "pK%d" % c, t % 2
        i0 = c * NC
        S, D, C = ("SROT%d" % P, i0, i0 + NC), ("D%d" % P, i0, i0 + NC), ("CH%d" % P, i0, i0 + NC)
        M, X, XS, CS, LI, LJ, OFF = [B("%s_%d" % (x, c)) for x in ("MASK", "X", "XS", "CS", "LI", "LJ", "OFF")]
        UZ, OH = ("pT%d" % c, 384, 512), ("pT%d" % c, 256, 384)
        tt(M, S, (K, zm, zm + NC), OP.is_le)
        if starts is None:
            tt(UZ, (K, zv, zv + NC), S, OP.subtract)
            mm((K, 384, 512), [(B("BLKb"), M)])
        else:
            mm((K, 384, 512), [(B("BLKb"), M)])
            starts()
            tt(UZ, (K, zv, zv + NC), S, OP.subtract)
        tt(X, UZ, D, OP.mult)
        ts(OH, (K, 384, 512), 1.0, OP.max, B("rp1"), OP.is_equal)
        tt(XS, OH, X, OP.mult)
        tt(CS, OH, C, OP.mult)
        mm((K, lreg, lreg + NC), [(B("BLKf"), XS), (B(mmc), CS)])
        ts(LI, (K, lreg, lreg + NC), B(col), OP.add)
        ts(LJ, LI, W - 1, AND)
        cp(OFF, LJ)

    def pick(t, c, dst, parts):
        a = 0
        for q, k in parts:
            gather(q, (dst, 16 * a, 16 * (a + k)), B("XL%d" % t), ("OFF_%d" % c, a, a + k))
            a += k

    for t in range(NV):
        P = t % 2
        last = t == NV - 1
        for c in range(2):
            E = "pE%d" % c
            tag[0] = "L%d" % c
            zs = (E, 128, 136)
            ts(B("ZL_%d" % c), zs, -16.0, OP.add, -float(ZC), OP.max)
            tt(B("DZ_%d" % c), zs, B("ZL_%d" % c), OP.subtract)
            lists(t, c, 0, 0, "MMC1", "rm8", 256)
        for c in range(2):
            tag[0] = "Y%d" % c
            mm(("pT%d" % c, 0, 256), [(B("IDb"), ("TT", 256 * c, 256 * c + 256))])
            pick(t, c, "Y_%d" % c, YSPLIT[c])
        for c in range(2):
            i0 = c * NC
            E, Y = "pE%d" % c, "Y_%d" % c
            er = (E, 0, 128)
            tag[0] = "M%d" % c
            mm(er, [(("TT", 256 * c, 256 * c + NC), B("BM%d" % c)), (("ONE", 0, 128, "p", 1), ("CROW", 0, 128, "p", 1))], True, False)
            for j in range(15 - JA[c]):
                for a in range(2):
                    s = (2 * j + a) * NC
                    tt(("MX_%d" % c, s, s + NC), ("pT%d" % c, 128 * a, 128 * a + 128), (Y, j + a, 16 * NC, 16), OP.max)
                    mm((E, j, 128, 16), [(("MX_%d" % c, s, s + NC), B("G32")), ((Y, j + a, 16 * NC, 16), B("GM16"))], False, False, er)
            for b in range(0, JA[c], 2):
                sl = [(j, a) for j in range(15 - JA[c] + b, min(15, 15 - JA[c] + b + 2)) for a in range(2)]
                pv = "p%s%d" % ("VK"[b // 2 % 2], c)
                tag[0] = "A%d" % c
                for k, (j, a) in enumerate(sl):
                    mm((pv, NC * k, NC * k + NC), [(B("IDb"), (Y, j + a, 16 * NC, 16)), (B("IDn"), ("TT", 256 * c + NC * a, 256 * c + NC * a + NC))])
                w, x = NC * len(sl), 2 * b * NC
                op("A", [lambda c=c, pv=pv, w=w, x=x: g.scalar.activation(T["AX_%d" % c][:, x:x + w], T[pv][:, 0:w], AF.Abs)],
                   [(pv, 0, w)], [("AX_%d" % c, x, x + w)], w)
                for k, (j, a) in enumerate(sl):
                    mm((E, j, 128, 16), [(("AX_%d" % c, x + NC * k, x + NC * k + NC), B("G16"))], False, False, er)
            tag[0] = "C%d" % c
            mm(er, [(("TT", 256 * c + NC, 256 * c + 2 * NC), B("BM%d" % c))], False, True)
            SC, KI, JJ, SM = [B("%s_%d" % (x, c)) for x in ("SC", "KI", "JJ", "SM")]
            op("V", [lambda c=c, E=E: g.vector.tensor_tensor_scan(T["SC_%d" % c][:, :], T.RST[:, :], T[E][:, 0:128], 1.0e9, OP.max, OP.min)],
               [er, B("RST")], [SC], 128)
            key = ("SC_%d" % c, 15, 128, 16)
            tie = ("SM_%d" % c, 16, 24)
            cp(KI, key)
            ts(tie, key, float(16 * TH), OP.is_lt)
            ts(JJ, KI, 15, AND)
            tt(B("TD_%d" % c), tie, B("DZ_%d" % c), OP.mult)
            tt(("SM_%d" % c, 8, 16), JJ, tie, OP.mult)
            tt(("SM_%d" % c, 0, 8), B("TD_%d" % c), B("ZL_%d" % c), OP.add)
            mm((E, 128, 256, "p", 24), [(SM, B("IDh"))])
            cp(("ST_%d" % c, 0, NC), (E, 128, 256, "p", 24))
            K = "pK%d" % c
            st = B("ST_%d" % c)
            for r, x in ((0, "EXz"), (128, "EXzn"), (256, "EXn")):
                mm((K, r, r + 128), [((x, 0, 128, "p", 24), st)])
            tag[0] = "R%d" % c

            def starts():
                tag[0] = "S%d" % c
                ts(B("GE_%d" % c), (K, 384, 512), B("rp1"), OP.is_le)
                gd = (E, 256, 384)
                tt(gd, B("GE_%d" % c), (K, 256, 384), OP.mult)
                tt(("SX%d" % t, i0, i0 + NC), ("SROT%d" % P, i0, i0 + NC), gd, OP.subtract)
                tag[0] = "Q%d" % c
            lists(t, c, 0, 128, "MMC2", "rr", 0, starts)
        for c in CORD:
            tag[0] = "S%d" % c
            lo, hi = c * NC, 257 if c else NC
            s = send(T.cores[(rank - 1) % n], ("SR%d" % (t + 1), lo, hi), ("SX%d" % t, lo, hi), "rs%d%d" % (t + 1, c), "ls%d%d" % (t + 1, c))
            recv(("SR%d" % (t + 1), lo, hi), T.cores[(rank + 1) % n], "rs%d%d" % (t + 1, c), RECV, s)
        if t < 2:
            send_log(t + 2)
        if not last:
            tag[0] = "P"
            an = ("pE1", 160, 168)
            mm(an, [(B("ONEh"), ("SM_0", 16, 24)), (B("ONEh"), ("SM_1", 16, 24))])
            tt(B("AP8"), an, B("G205"), OP.mult)
            acol = ("SX%d" % (t + 1), 256, 257)
            op("V", [lambda acol=acol: g.vector.tensor_reduce(ap(acol), T.AP8[:, :], AxisListType.X, OP.add)], [B("AP8")], [acol], 64)
            ts(B("LA"), B("i16"), acol, OP.add, 5.0, OP.mult)
            ts(B("LB"), B("LA"), 255, AND)
            cp(B("LO"), B("LB"))
            prep_c(t + 1, "A")
            tt(B("dA"), acol, ("SR%d" % (t + 1), 256, 257), OP.subtract)
            ts(B("LC"), B("i16"), B("dA"), OP.add)
            ts(B("LD"), B("LC"), 255, AND)
            cp(B("LS"), B("LD"))
            gather(DQ, B("SROT%d" % ((t + 1) % 2)), ("SR%d" % (t + 1), 0, 256), B("LS"))
        for c in range(2):
            tag[0] = "V%d" % c
            pick(t, c, "V_%d" % c, VSPLIT[c])
        for c in range(2):
            i0 = c * NC
            E, K, V, AB, st = "pE%d" % c, "pK%d" % c, "V_%d" % c, "AB_%d" % c, B("ST_%d" % c)
            for b in range(4):
                a = 512 * b
                tag[0] = "D%d" % c
                vd = ("p%s%d" % ("VT"[b % 2], c), 1, 512)
                mm(vd, [(B("IDb"), (V, a + 1, a + 512)), (B("IDn"), (V, a, a + 511))])
                op("A", [lambda AB=AB, a=a, vd=vd: g.scalar.activation(T[AB][:, a + 1:a + 512], ap(vd), AF.Abs)],
                   [vd], [(AB, a + 1, a + 512)], 512)
                if b % 2:
                    mm((E, 224 + 32 * b, 288 + 32 * b), [(("SEL", 128 * m, 128 * m + 128), (AB, 512 * b - 512 + m, 512 * b + 512, 16)) for m in range(2, 16)])
            tag[0] = "N%d" % c
            OV, IZ = B("OV_%d" % c), B("IZ_%d" % c)
            ts(OV, (E, 256, 384), float(TH2), OP.is_gt)
            mm((E, 384, 512), [(B("TRI"), OV)])
            ts(IZ, (E, 384, 512), 0.0, OP.is_equal)
            if last:
                mm((K, 0, NC, "p", 8), [(("EXs", 0, 8, "p", 24), st), (B("Gn"), IZ)])
            else:
                mm((K, 0, NC), [(("EXz", 0, 128, "p", 24), st), (B("BLKn"), IZ)])
            mm((E, 144, 152), [(("SEL", 128 * p, 128 * p + 128), ("IZ_%d" % c, p, NC, 16)) for p in range(16)] + [(B("IDb"), B("KT"))])
            if not last:
                mm((E, 128, 136), [(st, ("EXs", 0, 8, "p", 24)), (IZ, B("Gn"))])
            for a in range(2):
                ts(("TO_%d" % c, 8 * a, 8 * a + 8), (E, 144, 152), float(a - 2), OP.add)
            gather(TQ[c], ("TT", 256 * c, 256 * c + 256), B(V), B("TO_%d" % c))
            if last:
                ts(("YZ", i0, i0 + NC), (K, 0, NC, "p", 8), float(ZC), OP.add)
                for a in range(2):
                    x = ("TT", 256 * c + NC * a, 256 * c + NC * a + NC)
                    dma("SA"[a], T.yt[:, 256 * a + i0:256 * a + i0 + NC], ap(x), [x], [], "d_y%s%d" % ("ab"[a], c), 2500)
    dma("S", T.yz[:, :], T.YZ[:, :], [B("YZ")], [], "d_yz", 2000)
    ts(B("LC"), B("n205"), ("SR4", 256, 257), OP.subtract)
    ts(B("LD"), B("LC"), 255, AND)
    cp(B("LS"), B("LD"))
    gather("V", B("YSO"), ("SR4", 0, 256), B("LS"), 1.0, float(ZC))
    dma("S", T.ys[:, :], T.YSO[:, :], [B("YSO")], [], "d_ys", 2500)
    return ops


def link(ops):
    hist = {}
    for k, o in enumerate(ops):
        deps = {}

        def add(x, hard):
            deps[x] = deps.get(x, False) or hard
        if "after" in o:
            add(o["after"], False)
        acc = [(r, False) for r in o["r"]] + [(w, True) for w in o["w"]]
        for (b, lo, hi), wr in acc:
            ps = SCRATCH[b][0] == "psum"
            for (x, l2, h2, w2) in hist.get(b, ()):
                if x == k:
                    continue
                same = ops[x]["q"] == o["q"]
                if ps and (not same):
                    add(x, True)
                elif ps and o["q"] == "P":
                    add(x, False)
                elif (wr or w2) and lo < h2 and l2 < hi:
                    add(x, True)
        for (b, lo, hi), wr in acc:
            h = hist.setdefault(b, [])
            ps = SCRATCH[b][0] == "psum"
            if wr and not ps:
                h[:] = [y for y in h if not (lo <= y[1] and y[2] <= hi and y[0] != k)]
            if ps:
                h[:] = [y for y in h if ops[y[0]]["q"] != o["q"] or y[0] == k or (o["q"] != "P" and not (wr and lo <= y[1] and y[2] <= hi))] if o["q"] == "P" or wr else h
            h.append((k, lo, hi, wr))
        o["deps"] = deps


def order(ops):
    n = len(ops)
    succ = [[] for _ in range(n)]
    need = [0] * n
    for k, o in enumerate(ops):
        for x in o["deps"]:
            succ[x].append(k)
            need[k] += 1
    way = [0.0] * n
    for k in range(n - 1, -1, -1):
        way[k] = ops[k]["cost"] + SYNCNS + max([way[s] for s in succ[k]] + [0.0])
    for k, o in enumerate(ops):
        way[k] += BI.get(o["tag"], 0)
    prev = {}
    for k, o in enumerate(ops):
        if o["kind"] in ("dma", "send") or o["q"] == "G":
            if o["q"] in prev:
                succ[prev[o["q"]]].append(k)
                need[k] += 1
            prev[o["q"]] = k
    ready_at = [0.0] * n
    ready = {}
    free = {}
    seq = []

    def push(k):
        ready.setdefault(ops[k]["q"], []).append(k)
    for k in range(n):
        if need[k] == 0:
            push(k)
    while any(ready.values()):
        best = None
        for q, l in ready.items():
            if not l:
                continue
            f = free.get(q, 0.0) if q != "R" else 0.0
            t0 = max(f, min(ready_at[k] for k in l))
            k = min((k for k in l if ready_at[k] <= t0 + 1e-6), key=lambda k: (-way[k], k))
            if best is None or t0 < best[0]:
                best = (t0, q, k)
        t0, q, k = best
        ready[q].remove(k)
        o = ops[k]
        busy = {"dma": 60.0, "recv": 0.0, "send": o["cost"]}.get(o["kind"], o["cost"])
        free[q] = t0 + busy
        o["t0"] = t0
        end = t0 + o["cost"] + SYNCNS
        seq.append(k)
        for s in succ[k]:
            e = t0 + busy if (k not in ops[s]["deps"] or ops[s]["q"] == q and not ops[s]["deps"][k]) else end
            ready_at[s] = max(ready_at[s], e)
            need[s] -= 1
            if need[s] == 0:
                push(s)
    return seq


def emit(g, T, ops, seq):
    queue = {"V": g.vector, "A": g.scalar, "P": g.tensor, "G": g, "S": g.sync}
    total = {"V": 0, "A": 0, "P": 0, "G": 0}
    know = {q: {} for q in queue}
    waited = {}
    issued = []
    for k in seq:
        o = ops[k]
        q = o["q"]
        if o["kind"] == "recv":
            o["done"] = (o["sem"], o["cnt"])
            o["clock"] = {}
            issued.append(o["done"])
            continue
        eng = queue[q]
        for x in sorted(o["deps"], reverse=True):
            if not o["deps"][x]:
                continue
            d = ops[x]
            s, v = d["done"]
            if know[q].get(s, 0) >= v:
                continue
            eng.wait_ge(T.sem[s], v)
            waited[s] = max(waited.get(s, 0), v)
            know[q][s] = v
            for s2, v2 in d["clock"].items():
                if know[q].get(s2, 0) < v2:
                    know[q][s2] = v2
        if o["kind"] == "c":
            for f in o["fns"]:
                f().then_inc(T.sem["s" + q], 1)
            total[q] += len(o["fns"])
            o["done"] = ("s" + q, total[q])
        elif o["kind"] == "dma":
            for f in o["fns"]:
                f().then_inc(T.sem[o["sem"]], 16)
            o["done"] = (o["sem"], 16)
        else:
            for f in o["fns"]:
                f()
            o["done"] = (o["sem"], o["cnt"])
        o["clock"] = dict(know[q])
        if o["kind"] != "c":
            issued.append(o["done"])
    for q in total:
        if total[q]:
            issued.append(("s" + q, total[q]))
    for s, v in issued:
        if know["G"].get(s, 0) < v:
            g.wait_ge(T.sem[s], v)


def rank_program(g, core, T, topo):
    if T.rank_of(core) is None:
        return
    ops = plan(g, core, T, topo)
    link(ops)
    emit(g, T, ops, order(ops))
